import numpy as np
import ml_dtypes


def mxq(x, axis, fmt="e4m3"):
    dtype, down = {"e4m3": (ml_dtypes.float8_e4m3fn, 7), "e5m2": (ml_dtypes.float8_e5m2, 14)}[fmt]
    v = np.moveaxis(np.asarray(x, np.float32).astype(ml_dtypes.bfloat16).astype(np.float64), axis, -1)
    blocks = v.reshape(v.shape[:-1] + (-1, 32))
    amax = np.abs(blocks).max(-1, keepdims=True)
    byte = np.maximum(np.where(amax > 0, np.frexp(amax)[1] - 1 + 127, 0) - down, 1)
    scale = np.exp2(byte - 127.0)
    codes = (blocks / scale).astype(np.float32).astype(dtype).astype(np.float64)
    return np.moveaxis((codes * scale).reshape(v.shape), -1, axis)


WIDE = False


def mx_kscale(k):
    if not WIDE:
        return np.ones(k)
    levels = np.array([24, -24, 12, -12, 0])
    if k % 512:
        return np.exp2(np.random.permutation(np.resize(levels, k // 32))).repeat(32)
    a = np.empty((k // 512, 16))
    for p in range(k // 512):
        a[p, :8] = np.random.permutation(np.resize(levels, 8))
        for g in range(8):
            far = levels[np.abs(levels - a[p, g]) >= 10]
            a[p, g + 8] = far[np.random.randint(len(far))]
    return np.exp2(a.ravel()).repeat(32)


def f64(x):
    return np.asarray(x).astype(np.float64)


def striped(idx):
    return np.tile(idx.reshape(-1, 16).T, (8, 1)).astype(np.uint16)


def unstriped(offs):
    return offs[:16].T.reshape(-1).astype(np.int64)


E2M1 = np.array([0.0, 0.5, 1.0, 1.5, 2.0, 3.0, 4.0, 6.0, -0.0, -0.5, -1.0, -1.5, -2.0, -3.0, -4.0, -6.0])


def pack_weight(w, fmt):
    k, n = w.shape
    w = f64(np.asarray(w, np.float32).astype(ml_dtypes.bfloat16)).reshape(k // 32, 32, n)
    amax = np.abs(w).max(1)
    if fmt == "e4m3":
        byte = np.frexp(amax)[1] - 1 + 127 - 7
    else:
        mant, ex = np.frexp(amax / 6.0)
        byte = np.where(mant > 0.5, ex, ex - 1) + 127
    byte = np.clip(np.where(amax > 0, byte, 1), 1, 254)
    scaled = (w * np.exp2(127.0 - byte)[:, None, :]).reshape(k, n).astype(np.float32)
    by_word = np.ascontiguousarray(scaled.reshape(k // 512, 128, 4, n).transpose(0, 1, 3, 2))
    if fmt == "e4m3":
        words = by_word.astype(ml_dtypes.float8_e4m3fn).view(np.uint8)
    else:
        c = by_word.astype(ml_dtypes.float4_e2m1fn).view(np.uint8) & 0xF
        words = (c[..., 0::2] | (c[..., 1::2] << 4)).reshape(k // 512, 128, 2 * n)
    return np.ascontiguousarray(words), np.ascontiguousarray(byte.astype(np.uint8).reshape(k // 512, 16, n))


def unpack_weight(words, scales, fmt):
    g, _, n = scales.shape
    words = np.ascontiguousarray(words).reshape(g, 128, n, -1)
    if fmt == "e4m3":
        vals = words.view(ml_dtypes.float8_e4m3fn).astype(np.float64)
    else:
        nib = np.empty((g, 128, n, 4), np.uint8)
        nib[..., 0::2] = words & 0xF
        nib[..., 1::2] = words >> 4
        vals = E2M1[nib]
    vals = vals * np.repeat(np.exp2(scales.astype(np.float64) - 127.0), 8, axis=1)[..., None]
    return vals.transpose(0, 1, 3, 2).reshape(g * 512, n)


K, L, R, N, T, J = 512, 512, 512, 512, 4096, 2048


def setup_inputs():
    n = np.random.standard_normal
    s = mx_kscale(K)[:, None]
    s2 = mx_kscale(L)[:, None]
    u = mx_kscale(R)[:, None]
    p_tab = pack_weight(n((K, T)) * s, "e4m3")
    p_tab2 = pack_weight(n((L, T)) * s2, "e4m3")
    p_wrr = pack_weight(n((L, R)) / np.sqrt(L) / s2, "e2m1")
    p_wri = pack_weight(n((L, R)) / np.sqrt(L) / s2, "e2m1")
    return {
        "tab_words": p_tab[0],
        "tab_scales": p_tab[1],
        "tab2_words": p_tab2[0],
        "tab2_scales": p_tab2[1],
        "wer": (n((K, R)) / np.sqrt(K) / s * u.T).astype(np.float32),
        "wei": (n((K, R)) / np.sqrt(K) / s * u.T).astype(np.float32),
        "wrr_words": p_wrr[0],
        "wrr_scales": p_wrr[1],
        "wri_words": p_wri[0],
        "wri_scales": p_wri[1],
        "nr": (n((R, N)) / np.sqrt(R) / u).astype(np.float32),
        "ni": (n((R, N)) / np.sqrt(R) / u).astype(np.float32),
        "b": (0.3 * n(N)).astype(np.float32),
        "offs": striped(np.random.permutation(T)[:J]),
        "offs2": striped(np.random.permutation(T)[:J]),
    }


def reference(tab_words, tab_scales, tab2_words, tab2_scales, wer, wei, wrr_words, wrr_scales, wri_words, wri_scales, nr, ni, b, offs, offs2):
    idx = unstriped(offs)
    idx2 = unstriped(offs2)
    tab_ = unpack_weight(tab_words, tab_scales, "e4m3")[:, idx]
    tab2_ = unpack_weight(tab2_words, tab2_scales, "e4m3")[:, idx2]
    wer_ = mxq(f64(wer), 0, "e4m3")
    aer = wer_.T @ tab_
    wei_ = mxq(f64(wei), 0, "e4m3")
    aei = wei_.T @ tab_
    wrr_ = unpack_weight(wrr_words, wrr_scales, "e2m1")
    arr = wrr_.T @ tab2_
    wri_ = unpack_weight(wri_words, wri_scales, "e2m1")
    ari = wri_.T @ tab2_
    hr = aer * arr - aei * ari
    hi = aer * ari + aei * arr
    hr_ = mxq(hr, 0, "e4m3")
    hi_ = mxq(hi, 0, "e4m3")
    nr_ = mxq(f64(nr), 0, "e4m3")
    ni_ = mxq(f64(ni), 0, "e4m3")
    y = nr_.T @ hr_ + ni_.T @ hi_
    return y + f64(b)[:, None]

@@ -1,0 +1,217 @@
+from contextlib import ExitStack
+
+import concourse.mybir as mybir
+from concourse.masks import make_identity
+
+K, L, R, N, T, J = 512, 512, 512, 512, 4096, 2048
+FLOPS = 2 * J * (2 * K * R + 2 * L * R + 2 * R * N)
+
+F32 = mybir.dt.float32
+BF16 = mybir.dt.bfloat16
+I32 = mybir.dt.int32
+U32 = mybir.dt.uint32
+U16 = mybir.dt.uint16
+U8 = mybir.dt.uint8
+FP8X4 = mybir.dt.float8_e4m3fn_x4
+FP4X4 = mybir.dt.float4_e2m1fn_x4
+MULT = mybir.AluOpType.mult
+ADD = mybir.AluOpType.add
+COPY = mybir.ActivationFunctionType.Copy
+IDENT = mybir.ActivationFunctionType.Identity
+
+P = 128
+PACK = 4
+PICK = 512
+TILES = J // P
+SCORE_TILES = (4, 4, 4, 2, 1, 1)
+
+
+def tile_list_ckg_bias_kernel(
+    tc, tab_words, tab_scales, tab2_words, tab2_scales, wer, wei, wrr_words, wrr_scales,
+    wri_words, wri_scales, nr, ni, b, offs, offs2, out
+):
+    nc = tc.nc
+    with ExitStack() as ctx:
+        keep = ctx.enter_context(tc.tile_pool(name="keep", bufs=1))
+        ring = ctx.enter_context(tc.tile_pool(name="ring", bufs=2))
+        psum = ctx.enter_context(tc.psum_pool(name="psum", bufs=1))
+
+        list1 = keep.tile([P, J // 16], U16, name="list1")
+        list2 = keep.tile([P, J // 16], U16, name="list2")
+        words1 = keep.tile([P, T], U32, name="words1", align_bytes=64)
+        words2 = keep.tile([P, T], U32, name="words2", align_bytes=64)
+        planes1 = keep.tile([P, T], U8, name="planes1", align_bytes=64)
+        planes2 = keep.tile([P, T], U8, name="planes2", align_bytes=64)
+        wrr_codes = keep.tile([P, 2 * R], U8, name="wrr_codes", align_bytes=64)
+        wri_codes = keep.tile([P, 2 * R], U8, name="wri_codes", align_bytes=64)
+        wr_planes = keep.tile([P, 2 * R], U8, name="wr_planes", align_bytes=64)
+        bias = keep.tile([P, N // P], F32, name="bias")
+        identity = keep.tile([P, P], F32, name="identity", align_bytes=64)
+        warm = keep.tile([P, 2], F32, name="warm")
+
+        def load_scale_rows(queue, plane, rows):
+            for q in range(4):
+                queue.dma_start(out=plane.bitcast(I32)[32 * q : 32 * q + 4, :], in_=rows[0, 4 * q : 4 * q + 4, :].bitcast(I32))
+
+        def load_rows(weight):
+            raw = ring.tile([P, PACK, 512], F32, name="raw", align_bytes=64)
+            nc.sync.dma_start(out=raw[:], in_=weight.rearrange("(p i) c -> p i c", i=PACK))
+            return raw
+
+        nc.vector.memset(planes2[:].bitcast(I32), 0)
+        nc.gpsimd.memset(wr_planes[:].bitcast(I32), 0)
+        nc.vector.memset(planes1[:].bitcast(I32), 0)
+        nc.vector.memset(warm[:], 0.0)
+
+        nc.sync.dma_start(out=words2[:].bitcast(I32), in_=tab2_words[0].rearrange("p t i -> p (t i)").bitcast(I32))
+        nc.sync.dma_start(list2[:], offs2)
+        nc.sync.dma_start(out=wrr_codes[:].bitcast(I32), in_=wrr_words[0].bitcast(I32))
+        nc.sync.dma_start(out=wri_codes[:].bitcast(I32), in_=wri_words[0].bitcast(I32))
+        nc.sync.dma_start(list1[:], offs)
+        with nc.allow_non_contiguous_dma(reason="one bias value a partition"):
+            nc.sync.dma_start(out=bias[:], in_=b.rearrange("(c p) -> p c", p=P))
+        wer_raw = load_rows(wer)
+        wei_raw = load_rows(wei)
+        nc.sync.dma_start(out=words1[:].bitcast(I32), in_=tab_words[0].rearrange("p t i -> p (t i)").bitcast(I32))
+        load_scale_rows(nc.scalar, planes2[:], tab2_scales)
+        nc.scalar.activation(out=warm[:, 1:2], in_=warm[:, 0:1], func=IDENT, bias=warm[:, 0:1])
+        load_scale_rows(nc.gpsimd, wr_planes[:, 0:R], wrr_scales)
+        load_scale_rows(nc.gpsimd, wr_planes[:, R : 2 * R], wri_scales)
+        load_scale_rows(nc.sync, planes1[:], tab_scales)
+        make_identity(nc, identity[:])
+
+        def gather(words, planes, offsets, g, name, bufs):
+            cols = offsets[:, g * (PICK // 16) : (g + 1) * (PICK // 16)]
+            picked_words = ring.tile([P, PICK], U32, name=name + "_words", bufs=bufs, align_bytes=64)
+            picked_plane = ring.tile([P, PICK], U8, name=name + "_plane", bufs=bufs, align_bytes=64)
+            nc.vector.tensor_copy(picked_words[:], words[:].indirect(cols))
+            nc.vector.tensor_copy(picked_plane[:], planes[:].indirect(cols))
+            return picked_words, picked_plane
+
+        def quantise_weight(raw, name):
+            grouped = ring.tile([P, 512, PACK], BF16, name="grouped", align_bytes=64)
+            for half in range(2):
+                cols = slice(256 * half, 256 * (half + 1))
+                nc.scalar.copy(
+                    out=grouped[:, cols, :].rearrange("p (c e) i -> p c i e", e=4),
+                    in_=raw[:, :, cols].rearrange("p i (c e) -> p c i e", e=4),
+                )
+            codes = keep.tile([P, 512], U32, name=name + "_codes", align_bytes=64)
+            plane = keep.tile([P, 512], U8, name=name + "_plane", align_bytes=64)
+            nc.vector.quantize_mx(out=codes[:].bitcast(FP8X4), scales=plane[:], in_=grouped[:].rearrange("p c i -> p (c i)"))
+            return codes, plane
+
+        picked2 = [gather(words2, planes2, list2, g, "picked2", 4) for g in range(J // PICK)]
+        wer_q = quantise_weight(wer_raw, "wer")
+        wei_q = quantise_weight(wei_raw, "wei")
+        nr_raw = load_rows(nr)
+        ni_raw = load_rows(ni)
+        picked1 = {0: gather(words1, planes1, list1, 0, "picked1", 2)}
+
+        def project(picked, i, rhs, rhs_plane, tag, bufs):
+            cols = slice((i % 4) * P, (i % 4 + 1) * P)
+            bank = psum.tile([P, R], F32, name=tag, bufs=bufs)
+            nc.tensor.matmul_mx(
+                out=bank[:], lhsT=picked[0][:, cols].bitcast(FP8X4), lhsT_scale=picked[1][:, cols],
+                rhs=rhs, rhs_scale=rhs_plane, start=True, stop=True,
+            )
+            return bank[:].rearrange("p (m t) -> p t m", t=PACK)
+
+        def entity(i):
+            return [project(picked1[i // 4], i, w[0][:].bitcast(FP8X4), w[1][:], "ab", 3) for w in (wer_q, wei_q)]
+
+        def relation(i):
+            cd = ring.tile([P, 2, PACK, P], F32, name="cd", bufs=8, align_bytes=64)
+            for part, codes in enumerate((wrr_codes, wri_codes)):
+                bank = project(picked2[i // 4], i, codes[:].bitcast(FP4X4), wr_planes[:, part * R : (part + 1) * R], "cd_bank", 2)
+                nc.scalar.copy(out=cd[:, part], in_=bank)
+            return cd
+
+        def products(ab, cd):
+            a, bb = ab
+            prod = ring.tile([P, 4, PACK, P], F32, name="prod", bufs=3, align_bytes=64)
+            nc.vector.scalar_tensor_tensor(out=prod[:, 0], in0=a, scalar=-1.0, in1=cd[:, 0], op0=MULT, op1=MULT)
+            nc.vector.tensor_tensor(out=prod[:, 1], in0=a, in1=cd[:, 1], op=MULT)
+            nc.vector.tensor_tensor(out=prod[:, 2:4], in0=bb.unsqueeze(1).to_broadcast([P, 2, PACK, P]), in1=cd[:], op=MULT)
+            return prod
+
+        def turn_and_add(prod, h_bf16, place):
+            for part, (terms, sign) in enumerate((((3, 0), -1.0), ((2, 1), 1.0))):
+                bank = psum.tile([P, PACK, P], F32, name="h_bank", bufs=2)
+                for n_term, term in enumerate(terms):
+                    for t in range(PACK):
+                        nc.tensor.matmul(
+                            bank[:, t, :], lhsT=prod[:, term, t, :], rhs=identity[:], is_transpose=True,
+                            start=(n_term == 0 and t == 0), stop=(n_term == 1 and t == PACK - 1),
+                        )
+                nc.scalar.activation(
+                    out=h_bf16[:, part, place * P : (place + 1) * P, :], in_=bank[:].rearrange("p t j -> p j t"),
+                    func=COPY, scale=sign,
+                )
+
+        def quantise_h(h_bf16, width):
+            codes = ring.tile([P, 2, width], U32, name="h_codes", bufs=3, align_bytes=64)
+            plane = ring.tile([P, 2, width], U8, name="h_plane", bufs=3, align_bytes=64)
+            nc.vector.quantize_mx(
+                out=codes[:].rearrange("p s j -> p (s j)").bitcast(FP8X4), scales=plane[:].rearrange("p s j -> p (s j)"),
+                in_=h_bf16[:].rearrange("p s j t -> p (s j t)"),
+            )
+            return codes, plane
+
+        def score(h_q, j0, width, first, count, tag, bufs):
+            bank = psum.tile([P, count, width], F32, name=tag, bufs=bufs)
+            for c in range(count):
+                cols = slice((first + c) * P, (first + c + 1) * P)
+                for part, w in enumerate((nr_q, ni_q)):
+                    nc.tensor.matmul_mx(
+                        out=bank[:, c, :], lhsT=w[0][:, cols].bitcast(FP8X4), lhsT_scale=w[1][:, cols],
+                        rhs=h_q[0][:, part, :].bitcast(FP8X4), rhs_scale=h_q[1][:, part, :],
+                        start=(part == 0), stop=(part == 1),
+                    )
+            y = ring.tile([P, count, width], F32, name="y", bufs=4, align_bytes=64)
+            if count == 1:
+                nc.scalar.activation(out=y[:, 0, :], in_=bank[:, 0, :], func=IDENT, bias=bias[:, first : first + 1])
+            else:
+                nc.vector.tensor_tensor(
+                    out=y[:], in0=bank[:], in1=bias[:, first : first + count].unsqueeze(2).to_broadcast([P, count, width]), op=ADD
+                )
+            nc.sync.dma_start(
+                out=out[first * P : (first + count) * P, j0 : j0 + width].rearrange("(c p) j -> p c j", p=P), in_=y[:]
+            )
+
+        chunk_of = []
+        for c, n_tiles in enumerate(SCORE_TILES):
+            chunk_of.extend([(c, place, n_tiles) for place in range(n_tiles)])
+
+        waiting = []
+        ab = entity(0)
+        cd = relation(0)
+        for i in range(TILES):
+            c, place, n_tiles = chunk_of[i]
+            if i % 4 == 1 and i // 4 + 1 < J // PICK:
+                picked1[i // 4 + 1] = gather(words1, planes1, list1, i // 4 + 1, "picked1", 2)
+            if i == 1:
+                nr_q = quantise_weight(nr_raw, "nr")
+            if i == 2:
+                ni_q = quantise_weight(ni_raw, "ni")
+            ab_now, cd_now = ab, cd
+            if i + 1 < TILES:
+                ab = entity(i + 1)
+                cd = relation(i + 1)
+            prod = products(ab_now, cd_now)
+            if waiting:
+                score(*waiting[0], "y_bank", 1)
+                waiting = waiting[1:]
+            if waiting and i >= 13:
+                score(*waiting[0], "cd_bank", 2)
+                waiting = waiting[1:]
+            if place == 0:
+                h_bf16 = ring.tile([P, 2, n_tiles * P, PACK], BF16, name="h_bf16", align_bytes=64)
+            turn_and_add(prod, h_bf16, place)
+            if place == n_tiles - 1:
+                width = n_tiles * P
+                h_q = quantise_h(h_bf16, width)
+                count = 512 // width
+                waiting.extend([(h_q, (i + 1) * P - width, width, first, count) for first in range(0, N // P, count)])
+        for job in waiting:
+            score(*job, "cd_bank", 2)

@@ -23,6 +23,8 @@ P = 128
 PACK = 4
 PICK = 512
 TILES = J // P
+KINDS = "3333333333333330"
+SUB = mybir.AluOpType.subtract
 SCORE_TILES = (4, 4, 4, 2, 1, 1)
 
 
@@ -38,14 +40,12 @@ def tile_list_ckg_bias_kernel(
 
         list1 = keep.tile([P, J // 16], U16, name="list1")
         list2 = keep.tile([P, J // 16], U16, name="list2")
-        words1 = keep.tile([P, T], U32, name="words1", align_bytes=64)
         words2 = keep.tile([P, T], U32, name="words2", align_bytes=64)
         planes1 = keep.tile([P, T], U8, name="planes1", align_bytes=64)
         planes2 = keep.tile([P, T], U8, name="planes2", align_bytes=64)
         wrr_codes = keep.tile([P, 2 * R], U8, name="wrr_codes", align_bytes=64)
         wri_codes = keep.tile([P, 2 * R], U8, name="wri_codes", align_bytes=64)
         wr_planes = keep.tile([P, 2 * R], U8, name="wr_planes", align_bytes=64)
-        bias = keep.tile([P, N // P], F32, name="bias")
         identity = keep.tile([P, P], F32, name="identity", align_bytes=64)
         warm = keep.tile([P, 2], F32, name="warm")
 
@@ -53,32 +53,31 @@ def tile_list_ckg_bias_kernel(
             for q in range(4):
                 queue.dma_start(out=plane.bitcast(I32)[32 * q : 32 * q + 4, :], in_=rows[0, 4 * q : 4 * q + 4, :].bitcast(I32))
 
-        def load_rows(weight):
-            raw = ring.tile([P, PACK, 512], F32, name="raw", align_bytes=64)
-            nc.sync.dma_start(out=raw[:], in_=weight.rearrange("(p i) c -> p i c", i=PACK))
-            return raw
+        def load_rows(*weights):
+            raw = ring.tile([P, 2, PACK, 512], F32, name="raw", bufs=1, align_bytes=64)
+            for s, weight in enumerate(weights):
+                nc.sync.dma_start(out=raw[:, s], in_=weight.rearrange("(p i) c -> p i c", i=PACK))
+            return raw[:, 0], raw[:, 1]
 
         nc.vector.memset(planes2[:].bitcast(I32), 0)
-        nc.gpsimd.memset(wr_planes[:].bitcast(I32), 0)
+        nc.vector.memset(wr_planes[:].bitcast(I32), 0)
         nc.vector.memset(planes1[:].bitcast(I32), 0)
         nc.vector.memset(warm[:], 0.0)
-
-        nc.sync.dma_start(out=words2[:].bitcast(I32), in_=tab2_words[0].rearrange("p t i -> p (t i)").bitcast(I32))
-        nc.sync.dma_start(list2[:], offs2)
-        nc.sync.dma_start(out=wrr_codes[:].bitcast(I32), in_=wrr_words[0].bitcast(I32))
-        nc.sync.dma_start(out=wri_codes[:].bitcast(I32), in_=wri_words[0].bitcast(I32))
-        nc.sync.dma_start(list1[:], offs)
-        with nc.allow_non_contiguous_dma(reason="one bias value a partition"):
-            nc.sync.dma_start(out=bias[:], in_=b.rearrange("(c p) -> p c", p=P))
-        wer_raw = load_rows(wer)
-        wei_raw = load_rows(wei)
-        nc.sync.dma_start(out=words1[:].bitcast(I32), in_=tab_words[0].rearrange("p t i -> p (t i)").bitcast(I32))
-        load_scale_rows(nc.scalar, planes2[:], tab2_scales)
-        nc.scalar.activation(out=warm[:, 1:2], in_=warm[:, 0:1], func=IDENT, bias=warm[:, 0:1])
-        load_scale_rows(nc.gpsimd, wr_planes[:, 0:R], wrr_scales)
-        load_scale_rows(nc.gpsimd, wr_planes[:, R : 2 * R], wri_scales)
-        load_scale_rows(nc.sync, planes1[:], tab_scales)
         make_identity(nc, identity[:])
+        words1 = keep.tile([P, T], U32, name="words1", align_bytes=64)
+
+        nc.sync.dma_start(list2[:], offs2)
+        nc.sync.dma_start(list1[:], offs)
+        nc.scalar.dma_start(out=wrr_codes[:].bitcast(I32), in_=wrr_words[0].bitcast(I32))
+        nc.scalar.dma_start(out=wri_codes[:].bitcast(I32), in_=wri_words[0].bitcast(I32))
+        nc.sync.dma_start(out=words2[:].bitcast(I32), in_=tab2_words[0].rearrange("p t i -> p (t i)").bitcast(I32))
+        load_scale_rows(nc.scalar, planes2[:], tab2_scales)
+        wer_raw, wei_raw = load_rows(wer, wei)
+        load_scale_rows(nc.scalar, wr_planes[:, 0:R], wrr_scales)
+        load_scale_rows(nc.scalar, wr_planes[:, R : 2 * R], wri_scales)
+        nc.sync.dma_start(out=words1[:].bitcast(I32), in_=tab_words[0].rearrange("p t i -> p (t i)").bitcast(I32))
+        load_scale_rows(nc.gpsimd, planes1[:], tab_scales)
+        nc.scalar.activation(out=warm[:, 1:2], in_=warm[:, 0:1], func=IDENT, bias=warm[:, 0:1])
 
         def gather(words, planes, offsets, g, name, bufs):
             cols = offsets[:, g * (PICK // 16) : (g + 1) * (PICK // 16)]
@@ -88,25 +87,33 @@ def tile_list_ckg_bias_kernel(
             nc.vector.tensor_copy(picked_plane[:], planes[:].indirect(cols))
             return picked_words, picked_plane
 
-        def quantise_weight(raw, name):
-            grouped = ring.tile([P, 512, PACK], BF16, name="grouped", align_bytes=64)
+        def quantise_weight(raw, name, tag):
+            grouped = ring.tile([P, 512, PACK], BF16, name=tag, bufs=1, align_bytes=64)
             for half in range(2):
                 cols = slice(256 * half, 256 * (half + 1))
-                nc.scalar.copy(
-                    out=grouped[:, cols, :].rearrange("p (c e) i -> p c i e", e=4),
-                    in_=raw[:, :, cols].rearrange("p i (c e) -> p c i e", e=4),
-                )
+                if name in ("wer", "wei"):
+                    nc.scalar.copy(
+                        out=grouped[:, cols, :].rearrange("p (m e) i -> p m e i", e=2),
+                        in_=raw.rearrange("p i (m u e) -> p u m e i", u=2, e=2)[:, half],
+                    )
+                else:
+                    nc.scalar.copy(
+                        out=grouped[:, cols, :].rearrange("p (c e) i -> p c i e", e=4),
+                        in_=raw[:, :, cols].rearrange("p i (c e) -> p c i e", e=4),
+                    )
             codes = keep.tile([P, 512], U32, name=name + "_codes", align_bytes=64)
             plane = keep.tile([P, 512], U8, name=name + "_plane", align_bytes=64)
             nc.vector.quantize_mx(out=codes[:].bitcast(FP8X4), scales=plane[:], in_=grouped[:].rearrange("p c i -> p (c i)"))
             return codes, plane
 
-        picked2 = [gather(words2, planes2, list2, g, "picked2", 4) for g in range(J // PICK)]
-        wer_q = quantise_weight(wer_raw, "wer")
-        wei_q = quantise_weight(wei_raw, "wei")
-        nr_raw = load_rows(nr)
-        ni_raw = load_rows(ni)
-        picked1 = {0: gather(words1, planes1, list1, 0, "picked1", 2)}
+        picked2 = {g: gather(words2, planes2, list2, g, "picked", 4) for g in range(3)}
+        wer_q = quantise_weight(wer_raw, "wer", "spare0")
+        wei_q = quantise_weight(wei_raw, "wei", "spare1")
+        nr_raw, ni_raw = load_rows(nr, ni)
+        bias = ring.tile([P, N // P], F32, name="bias", bufs=1, align_bytes=64)
+        with nc.allow_non_contiguous_dma(reason="one bias value a partition"):
+            nc.gpsimd.dma_start(out=bias[:], in_=b.rearrange("(c p) -> p c", p=P))
+        picked1 = {0: gather(words1, planes1, list1, 0, "picked", 4)}
 
         def project(picked, i, rhs, rhs_plane, tag, bufs):
             cols = slice((i % 4) * P, (i % 4 + 1) * P)
@@ -115,33 +122,75 @@ def tile_list_ckg_bias_kernel(
                 out=bank[:], lhsT=picked[0][:, cols].bitcast(FP8X4), lhsT_scale=picked[1][:, cols],
                 rhs=rhs, rhs_scale=rhs_plane, start=True, stop=True,
             )
-            return bank[:].rearrange("p (m t) -> p t m", t=PACK)
+            return bank
 
         def entity(i):
-            return [project(picked1[i // 4], i, w[0][:].bitcast(FP8X4), w[1][:], "ab", 3) for w in (wer_q, wei_q)]
+            banks = [project(picked1[i // 4], i, w[0][:].bitcast(FP8X4), w[1][:], "ab", 3) for w in (wer_q, wei_q)]
+            if KINDS[i] == "3":
+                return [bank[:].unsqueeze(1).to_broadcast([P, 2, R]) for bank in banks]
+            a, bb = [bank[:].rearrange("p (w e) -> p e w", e=2) for bank in banks]
+            if KINDS[i] == "2":
+                a_sb = ring.tile([P, R], F32, name="a_sb", bufs=3, align_bytes=64)
+                nc.scalar.copy(out=halves(a_sb[:]), in_=a)
+                return a_sb, bb
+            return a, bb
+
+        def halves(x):
+            return x.rearrange("p (e w) -> p e w", e=2)
 
         def relation(i):
-            cd = ring.tile([P, 2, PACK, P], F32, name="cd", bufs=8, align_bytes=64)
+            cd = ring.tile([P, 2, R], F32, name="cd", bufs=3, align_bytes=64)
             for part, codes in enumerate((wrr_codes, wri_codes)):
                 bank = project(picked2[i // 4], i, codes[:].bitcast(FP4X4), wr_planes[:, part * R : (part + 1) * R], "cd_bank", 2)
-                nc.scalar.copy(out=cd[:, part], in_=bank)
+                if KINDS[i] == "3":
+                    nc.scalar.copy(out=cd[:, part].rearrange("p (u m e) -> p u m e", u=2, e=2), in_=bank[:].rearrange("p (m u e) -> p u m e", u=2, e=2))
+                else:
+                    nc.scalar.copy(out=cd[:, part].rearrange("p (e u m) -> p e u m", u=2, e=2), in_=bank[:].rearrange("p (m u e) -> p e u m", u=2, e=2))
             return cd
 
-        def products(ab, cd):
+        def products(ab, cd, i):
             a, bb = ab
-            prod = ring.tile([P, 4, PACK, P], F32, name="prod", bufs=3, align_bytes=64)
-            nc.vector.scalar_tensor_tensor(out=prod[:, 0], in0=a, scalar=-1.0, in1=cd[:, 0], op0=MULT, op1=MULT)
-            nc.vector.tensor_tensor(out=prod[:, 1], in0=a, in1=cd[:, 1], op=MULT)
-            nc.vector.tensor_tensor(out=prod[:, 2:4], in0=bb.unsqueeze(1).to_broadcast([P, 2, PACK, P]), in1=cd[:], op=MULT)
+            if i < 2:
+                prod = ring.tile([P, 4, R], F32, name="spare%d" % i, bufs=1, align_bytes=64)
+            else:
+                prod = ring.tile([P, 4, R], F32, name="prod", bufs=3, align_bytes=64)
+            if KINDS[i] == "0":
+                nc.vector.scalar_tensor_tensor(out=halves(prod[:, 0]), in0=a, scalar=-1.0, in1=halves(cd[:, 0]), op0=MULT, op1=MULT)
+                nc.vector.tensor_tensor(out=halves(prod[:, 1]), in0=a, in1=halves(cd[:, 1]), op=MULT)
+                nc.vector.tensor_tensor(
+                    out=prod[:, 2:4].rearrange("p s (e w) -> p s e w", e=2), in0=bb.unsqueeze(1).to_broadcast([P, 2, 2, R // 2]),
+                    in1=cd[:].rearrange("p s (e w) -> p s e w", e=2), op=MULT)
+            elif KINDS[i] == "2":
+                nc.gpsimd.tensor_tensor(out=prod[:, 0], in0=a[:], in1=cd[:, 0], op=MULT)
+                nc.gpsimd.tensor_tensor(out=prod[:, 1], in0=a[:], in1=cd[:, 1], op=MULT)
+                nc.vector.scalar_tensor_tensor(out=halves(prod[:, 3]), in0=bb, scalar=-1.0, in1=halves(cd[:, 1]), op0=MULT, op1=MULT)
+                nc.vector.tensor_tensor(out=halves(prod[:, 2]), in0=bb, in1=halves(cd[:, 0]), op=MULT)
+            else:
+                nc.vector.tensor_tensor(out=prod[:, 0:2], in0=a, in1=cd[:], op=MULT)
+                nc.vector.tensor_tensor(out=prod[:, 2:4], in0=bb, in1=cd[:], op=MULT)
             return prod
 
-        def turn_and_add(prod, h_bf16, place):
-            for part, (terms, sign) in enumerate((((3, 0), -1.0), ((2, 1), 1.0))):
+        def turn_and_add(prod, h_bf16, place, i):
+            if KINDS[i] == "3":
+                h_rows = ring.tile([P, 2, R], BF16, name="h_rows", bufs=2, align_bytes=64)
+                nc.gpsimd.tensor_tensor(out=h_rows[:, 1], in0=prod[:, 1], in1=prod[:, 2], op=ADD)
+                nc.gpsimd.tensor_tensor(out=h_rows[:, 0], in0=prod[:, 0], in1=prod[:, 3], op=SUB)
+                pairs = h_rows[:].rearrange("p s r -> p (s r)").bitcast(F32)
+                bank = psum.tile([P, PACK, P], F32, name="h_bank", bufs=2)
+                for block in range(4):
+                    nc.tensor.transpose(bank[:, block, :], pairs[:, block * P : (block + 1) * P], identity[:])
+                nc.scalar.copy(
+                    out=h_bf16[:, :, place * P : (place + 1) * P, :].bitcast(F32),
+                    in_=bank[:].rearrange("p (s u) j -> p s j u", u=2),
+                )
+                return
+            plan = (((3, 0), -1.0), ((2, 1), 1.0)) if KINDS[i] == "0" else (((0, 3), 1.0), ((1, 2), 1.0))
+            for part, (terms, sign) in enumerate(plan):
                 bank = psum.tile([P, PACK, P], F32, name="h_bank", bufs=2)
                 for n_term, term in enumerate(terms):
                     for t in range(PACK):
                         nc.tensor.matmul(
-                            bank[:, t, :], lhsT=prod[:, term, t, :], rhs=identity[:], is_transpose=True,
+                            bank[:, 2 * (t % 2) + t // 2, :], lhsT=prod[:, term, t * P : (t + 1) * P], rhs=identity[:], is_transpose=True,
                             start=(n_term == 0 and t == 0), stop=(n_term == 1 and t == PACK - 1),
                         )
                 nc.scalar.activation(
@@ -188,26 +237,28 @@ def tile_list_ckg_bias_kernel(
         cd = relation(0)
         for i in range(TILES):
             c, place, n_tiles = chunk_of[i]
-            if i % 4 == 1 and i // 4 + 1 < J // PICK:
-                picked1[i // 4 + 1] = gather(words1, planes1, list1, i // 4 + 1, "picked1", 2)
-            if i == 1:
-                nr_q = quantise_weight(nr_raw, "nr")
-            if i == 2:
-                ni_q = quantise_weight(ni_raw, "ni")
+            if i in (1, 5, 9):
+                picked1[i // 4 + 1] = gather(words1, planes1, list1, i // 4 + 1, "picked", 4)
+            if i == 8:
+                picked2[3] = gather(words2, planes2, list2, 3, "picked", 4)
             ab_now, cd_now = ab, cd
             if i + 1 < TILES:
                 ab = entity(i + 1)
                 cd = relation(i + 1)
-            prod = products(ab_now, cd_now)
+            prod = products(ab_now, cd_now, i)
             if waiting:
                 score(*waiting[0], "y_bank", 1)
                 waiting = waiting[1:]
-            if waiting and i >= 13:
+            if waiting and i >= 14:
                 score(*waiting[0], "cd_bank", 2)
                 waiting = waiting[1:]
             if place == 0:
                 h_bf16 = ring.tile([P, 2, n_tiles * P, PACK], BF16, name="h_bf16", align_bytes=64)
-            turn_and_add(prod, h_bf16, place)
+            turn_and_add(prod, h_bf16, place, i)
+            if i == 1:
+                nr_q = quantise_weight(nr_raw, "nr", "spare0")
+            if i == 2:
+                ni_q = quantise_weight(ni_raw, "ni", "spare1")
             if place == n_tiles - 1:
                 width = n_tiles * P
                 h_q = quantise_h(h_bf16, width)

@@ -23,7 +23,7 @@ P = 128
 PACK = 4
 PICK = 512
 TILES = J // P
-KINDS = "3333333333333330"
+KINDS = "0000000000000000"
 SUB = mybir.AluOpType.subtract
 SCORE_TILES = (4, 4, 4, 2, 1, 1)
 
@@ -49,8 +49,8 @@ def tile_list_ckg_bias_kernel(
         identity = keep.tile([P, P], F32, name="identity", align_bytes=64)
         warm = keep.tile([P, 2], F32, name="warm")
 
-        def load_scale_rows(queue, plane, rows):
-            for q in range(4):
+        def load_scale_rows(queue, plane, rows, quadrants=range(4)):
+            for q in quadrants:
                 queue.dma_start(out=plane.bitcast(I32)[32 * q : 32 * q + 4, :], in_=rows[0, 4 * q : 4 * q + 4, :].bitcast(I32))
 
         def load_rows(*weights):
@@ -68,24 +68,23 @@ def tile_list_ckg_bias_kernel(
 
         nc.sync.dma_start(list2[:], offs2)
         nc.sync.dma_start(list1[:], offs)
-        nc.scalar.dma_start(out=wrr_codes[:].bitcast(I32), in_=wrr_words[0].bitcast(I32))
-        nc.scalar.dma_start(out=wri_codes[:].bitcast(I32), in_=wri_words[0].bitcast(I32))
+        nc.sync.dma_start(out=wrr_codes[:].bitcast(I32), in_=wrr_words[0].bitcast(I32))
+        nc.sync.dma_start(out=wri_codes[:].bitcast(I32), in_=wri_words[0].bitcast(I32))
         nc.sync.dma_start(out=words2[:].bitcast(I32), in_=tab2_words[0].rearrange("p t i -> p (t i)").bitcast(I32))
-        load_scale_rows(nc.scalar, planes2[:], tab2_scales)
+        load_scale_rows(nc.scalar, planes2[:], tab2_scales, range(3))
+        load_scale_rows(nc.gpsimd, planes2[:], tab2_scales, range(3, 4))
         wer_raw, wei_raw = load_rows(wer, wei)
-        load_scale_rows(nc.scalar, wr_planes[:, 0:R], wrr_scales)
-        load_scale_rows(nc.scalar, wr_planes[:, R : 2 * R], wri_scales)
+        for q in range(4):
+            load_scale_rows(nc.scalar, wr_planes[:, 0:R], wrr_scales, [q])
+            load_scale_rows(nc.scalar, wr_planes[:, R : 2 * R], wri_scales, [q])
         nc.sync.dma_start(out=words1[:].bitcast(I32), in_=tab_words[0].rearrange("p t i -> p (t i)").bitcast(I32))
         load_scale_rows(nc.gpsimd, planes1[:], tab_scales)
         nc.scalar.activation(out=warm[:, 1:2], in_=warm[:, 0:1], func=IDENT, bias=warm[:, 0:1])
 
-        def gather(words, planes, offsets, g, name, bufs):
-            cols = offsets[:, g * (PICK // 16) : (g + 1) * (PICK // 16)]
-            picked_words = ring.tile([P, PICK], U32, name=name + "_words", bufs=bufs, align_bytes=64)
-            picked_plane = ring.tile([P, PICK], U8, name=name + "_plane", bufs=bufs, align_bytes=64)
-            nc.vector.tensor_copy(picked_words[:], words[:].indirect(cols))
-            nc.vector.tensor_copy(picked_plane[:], planes[:].indirect(cols))
-            return picked_words, picked_plane
+        def gather(window, offsets, g, dtype, tag):
+            picked = ring.tile([P, PICK], dtype, name=tag, bufs=1, align_bytes=64)
+            nc.vector.tensor_copy(picked[:], window[:].indirect(offsets[:, g * (PICK // 16) : (g + 1) * (PICK // 16)]))
+            return picked
 
         def quantise_weight(raw, name, tag):
             grouped = ring.tile([P, 512, PACK], BF16, name=tag, bufs=1, align_bytes=64)
@@ -106,14 +105,16 @@ def tile_list_ckg_bias_kernel(
             nc.vector.quantize_mx(out=codes[:].bitcast(FP8X4), scales=plane[:], in_=grouped[:].rearrange("p c i -> p (c i)"))
             return codes, plane
 
-        picked2 = {g: gather(words2, planes2, list2, g, "picked", 4) for g in range(3)}
+        plane2 = [gather(planes2, list2, g, U8, "plane%d" % g) for g in range(3)]
+        word2 = [gather(words2, list2, g, U32, "word%d" % g) for g in range(4)]
+        plane1 = [gather(planes1, list1, 0, U8, "plane3")]
         wer_q = quantise_weight(wer_raw, "wer", "spare0")
         wei_q = quantise_weight(wei_raw, "wei", "spare1")
         nr_raw, ni_raw = load_rows(nr, ni)
         bias = ring.tile([P, N // P], F32, name="bias", bufs=1, align_bytes=64)
         with nc.allow_non_contiguous_dma(reason="one bias value a partition"):
             nc.gpsimd.dma_start(out=bias[:], in_=b.rearrange("(c p) -> p c", p=P))
-        picked1 = {0: gather(words1, planes1, list1, 0, "picked", 4)}
+        word1 = [gather(words1, list1, 0, U32, "word4")]
 
         def project(picked, i, rhs, rhs_plane, tag, bufs):
             cols = slice((i % 4) * P, (i % 4 + 1) * P)
@@ -125,9 +126,9 @@ def tile_list_ckg_bias_kernel(
             return bank
 
         def entity(i):
-            banks = [project(picked1[i // 4], i, w[0][:].bitcast(FP8X4), w[1][:], "ab", 3) for w in (wer_q, wei_q)]
-            if KINDS[i] == "3":
-                return [bank[:].unsqueeze(1).to_broadcast([P, 2, R]) for bank in banks]
+            banks = [project((word1[i // 4], plane1[i // 4]), i, w[0][:].bitcast(FP8X4), w[1][:], "ab", 3) for w in (wer_q, wei_q)]
+            if KINDS[i] in "35":
+                return [bank[:] for bank in banks]
             a, bb = [bank[:].rearrange("p (w e) -> p e w", e=2) for bank in banks]
             if KINDS[i] == "2":
                 a_sb = ring.tile([P, R], F32, name="a_sb", bufs=3, align_bytes=64)
@@ -139,10 +140,10 @@ def tile_list_ckg_bias_kernel(
             return x.rearrange("p (e w) -> p e w", e=2)
 
         def relation(i):
-            cd = ring.tile([P, 2, R], F32, name="cd", bufs=3, align_bytes=64)
+            cd = ring.tile([P, 2, R], F32, name="cd", bufs=4, align_bytes=64)
             for part, codes in enumerate((wrr_codes, wri_codes)):
-                bank = project(picked2[i // 4], i, codes[:].bitcast(FP4X4), wr_planes[:, part * R : (part + 1) * R], "cd_bank", 2)
-                if KINDS[i] == "3":
+                bank = project((word2[i // 4], plane2[i // 4]), i, codes[:].bitcast(FP4X4), wr_planes[:, part * R : (part + 1) * R], "cd_bank", 2)
+                if KINDS[i] in "35":
                     nc.scalar.copy(out=cd[:, part].rearrange("p (u m e) -> p u m e", u=2, e=2), in_=bank[:].rearrange("p (m u e) -> p u m e", u=2, e=2))
                 else:
                     nc.scalar.copy(out=cd[:, part].rearrange("p (e u m) -> p e u m", u=2, e=2), in_=bank[:].rearrange("p (m u e) -> p e u m", u=2, e=2))
@@ -165,16 +166,23 @@ def tile_list_ckg_bias_kernel(
                 nc.gpsimd.tensor_tensor(out=prod[:, 1], in0=a[:], in1=cd[:, 1], op=MULT)
                 nc.vector.scalar_tensor_tensor(out=halves(prod[:, 3]), in0=bb, scalar=-1.0, in1=halves(cd[:, 1]), op0=MULT, op1=MULT)
                 nc.vector.tensor_tensor(out=halves(prod[:, 2]), in0=bb, in1=halves(cd[:, 0]), op=MULT)
+            elif KINDS[i] == "3":
+                nc.vector.tensor_tensor(out=prod[:, 0:2], in0=a.unsqueeze(1).to_broadcast([P, 2, R]), in1=cd[:], op=MULT)
+                nc.vector.tensor_tensor(out=prod[:, 2:4], in0=bb.unsqueeze(1).to_broadcast([P, 2, R]), in1=cd[:], op=MULT)
             else:
-                nc.vector.tensor_tensor(out=prod[:, 0:2], in0=a, in1=cd[:], op=MULT)
-                nc.vector.tensor_tensor(out=prod[:, 2:4], in0=bb, in1=cd[:], op=MULT)
+                nc.vector.tensor_tensor(out=prod[:, 0:2], in0=a.unsqueeze(1).to_broadcast([P, 2, R]), in1=cd[:], op=MULT)
+                nc.vector.scalar_tensor_tensor(out=prod[:, 2], in0=bb, scalar=-1.0, in1=cd[:, 1], op0=MULT, op1=MULT)
+                nc.vector.tensor_tensor(out=prod[:, 3], in0=bb, in1=cd[:, 0], op=MULT)
             return prod
 
         def turn_and_add(prod, h_bf16, place, i):
-            if KINDS[i] == "3":
+            if KINDS[i] in "35":
                 h_rows = ring.tile([P, 2, R], BF16, name="h_rows", bufs=2, align_bytes=64)
-                nc.gpsimd.tensor_tensor(out=h_rows[:, 1], in0=prod[:, 1], in1=prod[:, 2], op=ADD)
-                nc.gpsimd.tensor_tensor(out=h_rows[:, 0], in0=prod[:, 0], in1=prod[:, 3], op=SUB)
+                if KINDS[i] == "3":
+                    nc.gpsimd.tensor_tensor(out=h_rows[:, 1], in0=prod[:, 1], in1=prod[:, 2], op=ADD)
+                    nc.gpsimd.tensor_tensor(out=h_rows[:, 0], in0=prod[:, 0], in1=prod[:, 3], op=SUB)
+                else:
+                    nc.vector.tensor_tensor(out=h_rows[:], in0=prod[:, 0:2], in1=prod[:, 2:4], op=ADD)
                 pairs = h_rows[:].rearrange("p s r -> p (s r)").bitcast(F32)
                 bank = psum.tile([P, PACK, P], F32, name="h_bank", bufs=2)
                 for block in range(4):
@@ -233,25 +241,26 @@ def tile_list_ckg_bias_kernel(
             chunk_of.extend([(c, place, n_tiles) for place in range(n_tiles)])
 
         waiting = []
+        cds = [relation(i) for i in range(3)]
         ab = entity(0)
-        cd = relation(0)
         for i in range(TILES):
             c, place, n_tiles = chunk_of[i]
-            if i in (1, 5, 9):
-                picked1[i // 4 + 1] = gather(words1, planes1, list1, i // 4 + 1, "picked", 4)
-            if i == 8:
-                picked2[3] = gather(words2, planes2, list2, 3, "picked", 4)
-            ab_now, cd_now = ab, cd
+            ab_now = ab
+            if i % 4 == 3 and i + 1 < TILES:
+                word1.append(gather(words1, list1, i // 4 + 1, U32, "word4"))
+            if i in (1, 4, 8):
+                plane1.append(gather(planes1, list1, len(plane1), U8, "plane3" if i == 4 else "plane0"))
+            if i == 6:
+                plane2.append(gather(planes2, list2, 3, U8, "plane1"))
             if i + 1 < TILES:
                 ab = entity(i + 1)
-                cd = relation(i + 1)
-            prod = products(ab_now, cd_now, i)
-            if waiting:
-                score(*waiting[0], "y_bank", 1)
-                waiting = waiting[1:]
-            if waiting and i >= 14:
-                score(*waiting[0], "cd_bank", 2)
-                waiting = waiting[1:]
+            if i + 3 < TILES:
+                cds.append(relation(i + 3))
+            prod = products(ab_now, cds[i], i)
+            for tag, bufs in [("y_bank", 1), ("cd_bank", 2)][: 1 if i < 13 else 2]:
+                if waiting and waiting[0][0] + 2 <= i:
+                    score(*waiting[0][1:], tag, bufs)
+                    waiting = waiting[1:]
             if place == 0:
                 h_bf16 = ring.tile([P, 2, n_tiles * P, PACK], BF16, name="h_bf16", align_bytes=64)
             turn_and_add(prod, h_bf16, place, i)
@@ -263,6 +272,6 @@ def tile_list_ckg_bias_kernel(
                 width = n_tiles * P
                 h_q = quantise_h(h_bf16, width)
                 count = 512 // width
-                waiting.extend([(h_q, (i + 1) * P - width, width, first, count) for first in range(0, N // P, count)])
+                waiting.extend([(i, h_q, (i + 1) * P - width, width, first, count) for first in range(0, N // P, count)])
         for job in waiting:
-            score(*job, "cd_bank", 2)
+            score(*job[1:], "cd_bank", 2)

@@ -16,16 +16,23 @@ FP8X4 = mybir.dt.float8_e4m3fn_x4
 FP4X4 = mybir.dt.float4_e2m1fn_x4
 MULT = mybir.AluOpType.mult
 ADD = mybir.AluOpType.add
+SUBTRACT = mybir.AluOpType.subtract
 COPY = mybir.ActivationFunctionType.Copy
-IDENT = mybir.ActivationFunctionType.Identity
+IDENTITY = mybir.ActivationFunctionType.Identity
 
 P = 128
 PACK = 4
+BANK = 512
 PICK = 512
+PICK_TILES = PICK // P
+SLICES = J // PICK
 TILES = J // P
-KINDS = "0000000000000000"
-SUB = mybir.AluOpType.subtract
-SCORE_TILES = (4, 4, 4, 2, 1, 1)
+CHUNK_TILES = (4, 4, 4, 2, 1, 1)
+AHEAD = 2
+SCORE_LAG = 2
+VECTOR_SUM_FROM = 6
+VECTOR_SUM_EVERY = 3
+LENDING_TILES = (2, 3)
 
 
 def tile_list_ckg_bias_kernel(
@@ -38,173 +45,166 @@ def tile_list_ckg_bias_kernel(
         ring = ctx.enter_context(tc.tile_pool(name="ring", bufs=2))
         psum = ctx.enter_context(tc.psum_pool(name="psum", bufs=1))
 
-        list1 = keep.tile([P, J // 16], U16, name="list1")
-        list2 = keep.tile([P, J // 16], U16, name="list2")
-        words2 = keep.tile([P, T], U32, name="words2", align_bytes=64)
-        planes1 = keep.tile([P, T], U8, name="planes1", align_bytes=64)
-        planes2 = keep.tile([P, T], U8, name="planes2", align_bytes=64)
+        entity_list = keep.tile([P, J // 16], U16, name="entity_list")
+        relation_list = keep.tile([P, J // 16], U16, name="relation_list")
+        relation_words = keep.tile([P, T], U32, name="relation_words", align_bytes=64)
+        entity_plane = keep.tile([P, T], U8, name="entity_plane", align_bytes=64)
+        relation_plane = keep.tile([P, T], U8, name="relation_plane", align_bytes=64)
         wrr_codes = keep.tile([P, 2 * R], U8, name="wrr_codes", align_bytes=64)
         wri_codes = keep.tile([P, 2 * R], U8, name="wri_codes", align_bytes=64)
         wr_planes = keep.tile([P, 2 * R], U8, name="wr_planes", align_bytes=64)
         identity = keep.tile([P, P], F32, name="identity", align_bytes=64)
-        warm = keep.tile([P, 2], F32, name="warm")
+        entity_words = keep.tile([P, T], U32, name="entity_words", align_bytes=64)
 
-        def load_scale_rows(queue, plane, rows, quadrants=range(4)):
-            for q in quadrants:
-                queue.dma_start(out=plane.bitcast(I32)[32 * q : 32 * q + 4, :], in_=rows[0, 4 * q : 4 * q + 4, :].bitcast(I32))
+        def load_scale_rows(plane, rows, quadrant):
+            nc.scalar.dma_start(
+                out=plane.bitcast(I32)[32 * quadrant : 32 * quadrant + 4, :],
+                in_=rows[0, 4 * quadrant : 4 * quadrant + 4, :].bitcast(I32),
+            )
 
-        def load_rows(*weights):
-            raw = ring.tile([P, 2, PACK, 512], F32, name="raw", bufs=1, align_bytes=64)
-            for s, weight in enumerate(weights):
-                nc.sync.dma_start(out=raw[:, s], in_=weight.rearrange("(p i) c -> p i c", i=PACK))
-            return raw[:, 0], raw[:, 1]
+        def load_words(words, table):
+            nc.sync.dma_start(out=words[:].bitcast(I32), in_=table[0].rearrange("p t i -> p (t i)").bitcast(I32))
 
-        nc.vector.memset(planes2[:].bitcast(I32), 0)
+        def load_rows(weight):
+            raw = ring.tile([P, PACK, 512], F32, name="raw", align_bytes=64)
+            nc.sync.dma_start(out=raw[:], in_=weight.rearrange("(p i) c -> p i c", i=PACK))
+            return raw
+
+        nc.vector.memset(relation_plane[:].bitcast(I32), 0)
         nc.vector.memset(wr_planes[:].bitcast(I32), 0)
-        nc.vector.memset(planes1[:].bitcast(I32), 0)
-        nc.vector.memset(warm[:], 0.0)
+        nc.vector.memset(entity_plane[:].bitcast(I32), 0)
         make_identity(nc, identity[:])
-        words1 = keep.tile([P, T], U32, name="words1", align_bytes=64)
 
-        nc.sync.dma_start(list2[:], offs2)
-        nc.sync.dma_start(list1[:], offs)
+        nc.sync.dma_start(relation_list[:], offs2)
+        nc.sync.dma_start(entity_list[:], offs)
         nc.sync.dma_start(out=wrr_codes[:].bitcast(I32), in_=wrr_words[0].bitcast(I32))
         nc.sync.dma_start(out=wri_codes[:].bitcast(I32), in_=wri_words[0].bitcast(I32))
-        nc.sync.dma_start(out=words2[:].bitcast(I32), in_=tab2_words[0].rearrange("p t i -> p (t i)").bitcast(I32))
-        load_scale_rows(nc.scalar, planes2[:], tab2_scales, range(3))
-        load_scale_rows(nc.gpsimd, planes2[:], tab2_scales, range(3, 4))
-        wer_raw, wei_raw = load_rows(wer, wei)
-        for q in range(4):
-            load_scale_rows(nc.scalar, wr_planes[:, 0:R], wrr_scales, [q])
-            load_scale_rows(nc.scalar, wr_planes[:, R : 2 * R], wri_scales, [q])
-        nc.sync.dma_start(out=words1[:].bitcast(I32), in_=tab_words[0].rearrange("p t i -> p (t i)").bitcast(I32))
-        load_scale_rows(nc.gpsimd, planes1[:], tab_scales)
-        nc.scalar.activation(out=warm[:, 1:2], in_=warm[:, 0:1], func=IDENT, bias=warm[:, 0:1])
+        load_words(relation_words, tab2_words)
+        for quadrant in range(4):
+            load_scale_rows(relation_plane[:], tab2_scales, quadrant)
+        wer_raw = load_rows(wer)
+        wei_raw = load_rows(wei)
+        for quadrant in range(4):
+            load_scale_rows(wr_planes[:, 0:R], wrr_scales, quadrant)
+            load_scale_rows(wr_planes[:, R : 2 * R], wri_scales, quadrant)
+        for quadrant in range(4):
+            load_scale_rows(entity_plane[:], tab_scales, quadrant)
+        load_words(entity_words, tab_words)
 
-        def gather(window, offsets, g, dtype, tag):
-            picked = ring.tile([P, PICK], dtype, name=tag, bufs=1, align_bytes=64)
+        def gather(window, offsets, g, dtype, buffer):
+            picked = ring.tile([P, PICK], dtype, name=buffer, bufs=1, align_bytes=64)
             nc.vector.tensor_copy(picked[:], window[:].indirect(offsets[:, g * (PICK // 16) : (g + 1) * (PICK // 16)]))
             return picked
 
-        def quantise_weight(raw, name, tag):
-            grouped = ring.tile([P, 512, PACK], BF16, name=tag, bufs=1, align_bytes=64)
+        def quantise_weight(raw, name, buffer):
+            grouped = ring.tile([P, 512, PACK], BF16, name=buffer, bufs=1, align_bytes=64)
             for half in range(2):
                 cols = slice(256 * half, 256 * (half + 1))
-                if name in ("wer", "wei"):
-                    nc.scalar.copy(
-                        out=grouped[:, cols, :].rearrange("p (m e) i -> p m e i", e=2),
-                        in_=raw.rearrange("p i (m u e) -> p u m e i", u=2, e=2)[:, half],
-                    )
-                else:
-                    nc.scalar.copy(
-                        out=grouped[:, cols, :].rearrange("p (c e) i -> p c i e", e=4),
-                        in_=raw[:, :, cols].rearrange("p i (c e) -> p c i e", e=4),
-                    )
+                nc.scalar.copy(
+                    out=grouped[:, cols, :].rearrange("p (c e) i -> p c i e", e=4),
+                    in_=raw[:, :, cols].rearrange("p i (c e) -> p c i e", e=4),
+                )
             codes = keep.tile([P, 512], U32, name=name + "_codes", align_bytes=64)
             plane = keep.tile([P, 512], U8, name=name + "_plane", align_bytes=64)
-            nc.vector.quantize_mx(out=codes[:].bitcast(FP8X4), scales=plane[:], in_=grouped[:].rearrange("p c i -> p (c i)"))
+            nc.vector.quantize_mx(
+                out=codes[:].bitcast(FP8X4), scales=plane[:], in_=grouped[:].rearrange("p c i -> p (c i)")
+            )
             return codes, plane
 
-        plane2 = [gather(planes2, list2, g, U8, "plane%d" % g) for g in range(3)]
-        word2 = [gather(words2, list2, g, U32, "word%d" % g) for g in range(4)]
-        plane1 = [gather(planes1, list1, 0, U8, "plane3")]
-        wer_q = quantise_weight(wer_raw, "wer", "spare0")
-        wei_q = quantise_weight(wei_raw, "wei", "spare1")
-        nr_raw, ni_raw = load_rows(nr, ni)
+        relation_scales = [gather(relation_plane, relation_list, g, U8, "scales%d" % g) for g in range(SLICES - 1)]
+        relation_picked = [gather(relation_words, relation_list, g, U32, "relation%d" % g) for g in range(SLICES)]
+        entity_scales = [gather(entity_plane, entity_list, 0, U8, "scales_even")]
+        wer_q = quantise_weight(wer_raw, "wer", "lent0")
+        wei_q = quantise_weight(wei_raw, "wei", "lent1")
+        nr_raw = load_rows(nr)
+        ni_raw = load_rows(ni)
         bias = ring.tile([P, N // P], F32, name="bias", bufs=1, align_bytes=64)
         with nc.allow_non_contiguous_dma(reason="one bias value a partition"):
-            nc.gpsimd.dma_start(out=bias[:], in_=b.rearrange("(c p) -> p c", p=P))
-        word1 = [gather(words1, list1, 0, U32, "word4")]
+            nc.sync.dma_start(out=bias[:], in_=b.rearrange("(c p) -> p c", p=P))
+        entity_picked = [gather(entity_words, entity_list, 0, U32, "entity")]
 
-        def project(picked, i, rhs, rhs_plane, tag, bufs):
-            cols = slice((i % 4) * P, (i % 4 + 1) * P)
-            bank = psum.tile([P, R], F32, name=tag, bufs=bufs)
+        def sums_on_vector(i):
+            return i >= VECTOR_SUM_FROM and i % VECTOR_SUM_EVERY == 0
+
+        def project(words, scales, i, weight, weight_plane, bank_name, bufs):
+            cols = slice((i % PICK_TILES) * P, (i % PICK_TILES + 1) * P)
+            bank = psum.tile([P, R], F32, name=bank_name, bufs=bufs)
             nc.tensor.matmul_mx(
-                out=bank[:], lhsT=picked[0][:, cols].bitcast(FP8X4), lhsT_scale=picked[1][:, cols],
-                rhs=rhs, rhs_scale=rhs_plane, start=True, stop=True,
+                out=bank[:], lhsT=words[i // PICK_TILES][:, cols].bitcast(FP8X4), lhsT_scale=scales[i // PICK_TILES][:, cols],
+                rhs=weight, rhs_scale=weight_plane, start=True, stop=True,
             )
             return bank
 
         def entity(i):
-            banks = [project((word1[i // 4], plane1[i // 4]), i, w[0][:].bitcast(FP8X4), w[1][:], "ab", 3) for w in (wer_q, wei_q)]
-            if KINDS[i] in "35":
-                return [bank[:] for bank in banks]
-            a, bb = [bank[:].rearrange("p (w e) -> p e w", e=2) for bank in banks]
-            if KINDS[i] == "2":
-                a_sb = ring.tile([P, R], F32, name="a_sb", bufs=3, align_bytes=64)
-                nc.scalar.copy(out=halves(a_sb[:]), in_=a)
-                return a_sb, bb
-            return a, bb
+            return [
+                project(entity_picked, entity_scales, i, codes[:].bitcast(FP8X4), plane[:], "ab_bank", 3)
+                for codes, plane in (wer_q, wei_q)
+            ]
 
-        def halves(x):
-            return x.rearrange("p (e w) -> p e w", e=2)
+        def from_bank(bank, i):
+            if sums_on_vector(i):
+                return bank[:].rearrange("p (m u e) -> p u m e", u=2, e=2)
+            return bank[:].rearrange("p (m t) -> p t m", t=PACK)
+
+        def as_stored(row, i):
+            if sums_on_vector(i):
+                return row.rearrange("p (u m e) -> p u m e", u=2, e=2)
+            return row.rearrange("p (t m) -> p t m", t=PACK)
 
         def relation(i):
-            cd = ring.tile([P, 2, R], F32, name="cd", bufs=4, align_bytes=64)
+            if i == 0:
+                cd = ring.tile([P, 2, R], F32, name="scales_odd", bufs=1, align_bytes=64)
+            else:
+                cd = ring.tile([P, 2, R], F32, name="cd", bufs=AHEAD + 1, align_bytes=64)
             for part, codes in enumerate((wrr_codes, wri_codes)):
-                bank = project((word2[i // 4], plane2[i // 4]), i, codes[:].bitcast(FP4X4), wr_planes[:, part * R : (part + 1) * R], "cd_bank", 2)
-                if KINDS[i] in "35":
-                    nc.scalar.copy(out=cd[:, part].rearrange("p (u m e) -> p u m e", u=2, e=2), in_=bank[:].rearrange("p (m u e) -> p u m e", u=2, e=2))
-                else:
-                    nc.scalar.copy(out=cd[:, part].rearrange("p (e u m) -> p e u m", u=2, e=2), in_=bank[:].rearrange("p (m u e) -> p e u m", u=2, e=2))
+                bank = project(
+                    relation_picked, relation_scales, i, codes[:].bitcast(FP4X4),
+                    wr_planes[:, part * R : (part + 1) * R], "cd_bank", 2,
+                )
+                nc.scalar.copy(out=as_stored(cd[:, part], i), in_=from_bank(bank, i))
             return cd
 
         def products(ab, cd, i):
-            a, bb = ab
-            if i < 2:
-                prod = ring.tile([P, 4, R], F32, name="spare%d" % i, bufs=1, align_bytes=64)
+            a_view, b_view = [from_bank(bank, i) for bank in ab]
+            if i in LENDING_TILES:
+                prod = ring.tile([P, 4, R], F32, name="lent%d" % LENDING_TILES.index(i), bufs=1, align_bytes=64)
             else:
                 prod = ring.tile([P, 4, R], F32, name="prod", bufs=3, align_bytes=64)
-            if KINDS[i] == "0":
-                nc.vector.scalar_tensor_tensor(out=halves(prod[:, 0]), in0=a, scalar=-1.0, in1=halves(cd[:, 0]), op0=MULT, op1=MULT)
-                nc.vector.tensor_tensor(out=halves(prod[:, 1]), in0=a, in1=halves(cd[:, 1]), op=MULT)
-                nc.vector.tensor_tensor(
-                    out=prod[:, 2:4].rearrange("p s (e w) -> p s e w", e=2), in0=bb.unsqueeze(1).to_broadcast([P, 2, 2, R // 2]),
-                    in1=cd[:].rearrange("p s (e w) -> p s e w", e=2), op=MULT)
-            elif KINDS[i] == "2":
-                nc.gpsimd.tensor_tensor(out=prod[:, 0], in0=a[:], in1=cd[:, 0], op=MULT)
-                nc.gpsimd.tensor_tensor(out=prod[:, 1], in0=a[:], in1=cd[:, 1], op=MULT)
-                nc.vector.scalar_tensor_tensor(out=halves(prod[:, 3]), in0=bb, scalar=-1.0, in1=halves(cd[:, 1]), op0=MULT, op1=MULT)
-                nc.vector.tensor_tensor(out=halves(prod[:, 2]), in0=bb, in1=halves(cd[:, 0]), op=MULT)
-            elif KINDS[i] == "3":
-                nc.vector.tensor_tensor(out=prod[:, 0:2], in0=a.unsqueeze(1).to_broadcast([P, 2, R]), in1=cd[:], op=MULT)
-                nc.vector.tensor_tensor(out=prod[:, 2:4], in0=bb.unsqueeze(1).to_broadcast([P, 2, R]), in1=cd[:], op=MULT)
+            if sums_on_vector(i):
+                for term, (view, part) in enumerate(((a_view, 0), (a_view, 1), (b_view, 0), (b_view, 1))):
+                    nc.vector.tensor_tensor(out=as_stored(prod[:, term], i), in0=view, in1=as_stored(cd[:, part], i), op=MULT)
             else:
-                nc.vector.tensor_tensor(out=prod[:, 0:2], in0=a.unsqueeze(1).to_broadcast([P, 2, R]), in1=cd[:], op=MULT)
-                nc.vector.scalar_tensor_tensor(out=prod[:, 2], in0=bb, scalar=-1.0, in1=cd[:, 1], op0=MULT, op1=MULT)
-                nc.vector.tensor_tensor(out=prod[:, 3], in0=bb, in1=cd[:, 0], op=MULT)
+                nc.vector.scalar_tensor_tensor(
+                    out=as_stored(prod[:, 0], i), in0=a_view, scalar=-1.0, in1=as_stored(cd[:, 0], i), op0=MULT, op1=MULT
+                )
+                nc.vector.tensor_tensor(out=as_stored(prod[:, 1], i), in0=a_view, in1=as_stored(cd[:, 1], i), op=MULT)
+                nc.vector.tensor_tensor(
+                    out=prod[:, 2:4].rearrange("p s (t m) -> p s t m", t=PACK),
+                    in0=b_view.unsqueeze(1).to_broadcast([P, 2, PACK, P]),
+                    in1=cd[:].rearrange("p s (t m) -> p s t m", t=PACK), op=MULT,
+                )
             return prod
 
-        def turn_and_add(prod, h_bf16, place, i):
-            if KINDS[i] in "35":
-                h_rows = ring.tile([P, 2, R], BF16, name="h_rows", bufs=2, align_bytes=64)
-                if KINDS[i] == "3":
-                    nc.gpsimd.tensor_tensor(out=h_rows[:, 1], in0=prod[:, 1], in1=prod[:, 2], op=ADD)
-                    nc.gpsimd.tensor_tensor(out=h_rows[:, 0], in0=prod[:, 0], in1=prod[:, 3], op=SUB)
-                else:
-                    nc.vector.tensor_tensor(out=h_rows[:], in0=prod[:, 0:2], in1=prod[:, 2:4], op=ADD)
+        def add_and_turn(prod, h_slot, i):
+            if sums_on_vector(i):
+                h_rows = ring.tile([P, 2, R], BF16, name="h_rows", align_bytes=64)
+                nc.vector.tensor_tensor(out=h_rows[:, 1], in0=prod[:, 1], in1=prod[:, 2], op=ADD)
+                nc.vector.tensor_tensor(out=h_rows[:, 0], in0=prod[:, 0], in1=prod[:, 3], op=SUBTRACT)
                 pairs = h_rows[:].rearrange("p s r -> p (s r)").bitcast(F32)
                 bank = psum.tile([P, PACK, P], F32, name="h_bank", bufs=2)
                 for block in range(4):
                     nc.tensor.transpose(bank[:, block, :], pairs[:, block * P : (block + 1) * P], identity[:])
-                nc.scalar.copy(
-                    out=h_bf16[:, :, place * P : (place + 1) * P, :].bitcast(F32),
-                    in_=bank[:].rearrange("p (s u) j -> p s j u", u=2),
-                )
+                nc.scalar.copy(out=h_slot.bitcast(F32), in_=bank[:].rearrange("p (s u) j -> p s j u", u=2))
                 return
-            plan = (((3, 0), -1.0), ((2, 1), 1.0)) if KINDS[i] == "0" else (((0, 3), 1.0), ((1, 2), 1.0))
-            for part, (terms, sign) in enumerate(plan):
+            for part, (terms, sign) in enumerate((((3, 0), -1.0), ((2, 1), 1.0))):
                 bank = psum.tile([P, PACK, P], F32, name="h_bank", bufs=2)
                 for n_term, term in enumerate(terms):
                     for t in range(PACK):
                         nc.tensor.matmul(
-                            bank[:, 2 * (t % 2) + t // 2, :], lhsT=prod[:, term, t * P : (t + 1) * P], rhs=identity[:], is_transpose=True,
+                            bank[:, t, :], lhsT=prod[:, term, t * P : (t + 1) * P], rhs=identity[:], is_transpose=True,
                             start=(n_term == 0 and t == 0), stop=(n_term == 1 and t == PACK - 1),
                         )
-                nc.scalar.activation(
-                    out=h_bf16[:, part, place * P : (place + 1) * P, :], in_=bank[:].rearrange("p t j -> p j t"),
-                    func=COPY, scale=sign,
-                )
+                nc.scalar.activation(out=h_slot[:, part], in_=bank[:].rearrange("p t j -> p j t"), func=COPY, scale=sign)
 
         def quantise_h(h_bf16, width):
             codes = ring.tile([P, 2, width], U32, name="h_codes", bufs=3, align_bytes=64)
@@ -215,19 +215,23 @@ def tile_list_ckg_bias_kernel(
             )
             return codes, plane
 
-        def score(h_q, j0, width, first, count, tag, bufs):
-            bank = psum.tile([P, count, width], F32, name=tag, bufs=bufs)
+        def score(h_q, j0, width, first, bank_name, bufs):
+            count = BANK // width
+            bank = psum.tile([P, count, width], F32, name=bank_name, bufs=bufs)
             for c in range(count):
                 cols = slice((first + c) * P, (first + c + 1) * P)
-                for part, w in enumerate((nr_q, ni_q)):
+                for part, (codes, plane) in enumerate((nr_q, ni_q)):
                     nc.tensor.matmul_mx(
-                        out=bank[:, c, :], lhsT=w[0][:, cols].bitcast(FP8X4), lhsT_scale=w[1][:, cols],
+                        out=bank[:, c, :], lhsT=codes[:, cols].bitcast(FP8X4), lhsT_scale=plane[:, cols],
                         rhs=h_q[0][:, part, :].bitcast(FP8X4), rhs_scale=h_q[1][:, part, :],
                         start=(part == 0), stop=(part == 1),
                     )
             y = ring.tile([P, count, width], F32, name="y", bufs=4, align_bytes=64)
-            if count == 1:
-                nc.scalar.activation(out=y[:, 0, :], in_=bank[:, 0, :], func=IDENT, bias=bias[:, first : first + 1])
+            if j0 + width < J:
+                for c in range(count):
+                    nc.scalar.activation(
+                        out=y[:, c, :], in_=bank[:, c, :], func=IDENTITY, bias=bias[:, first + c : first + c + 1]
+                    )
             else:
                 nc.vector.tensor_tensor(
                     out=y[:], in0=bank[:], in1=bias[:, first : first + count].unsqueeze(2).to_broadcast([P, count, width]), op=ADD
@@ -236,42 +240,43 @@ def tile_list_ckg_bias_kernel(
                 out=out[first * P : (first + count) * P, j0 : j0 + width].rearrange("(c p) j -> p c j", p=P), in_=y[:]
             )
 
-        chunk_of = []
-        for c, n_tiles in enumerate(SCORE_TILES):
-            chunk_of.extend([(c, place, n_tiles) for place in range(n_tiles)])
+        place_of = []
+        for n_tiles in CHUNK_TILES:
+            place_of.extend([(place, n_tiles) for place in range(n_tiles)])
 
         waiting = []
-        cds = [relation(i) for i in range(3)]
-        ab = entity(0)
+        cds = [relation(i) for i in range(AHEAD)]
+        ab_next = entity(0)
         for i in range(TILES):
-            c, place, n_tiles = chunk_of[i]
-            ab_now = ab
-            if i % 4 == 3 and i + 1 < TILES:
-                word1.append(gather(words1, list1, i // 4 + 1, U32, "word4"))
-            if i in (1, 4, 8):
-                plane1.append(gather(planes1, list1, len(plane1), U8, "plane3" if i == 4 else "plane0"))
-            if i == 6:
-                plane2.append(gather(planes2, list2, 3, U8, "plane1"))
+            place, n_tiles = place_of[i]
+            g = i // PICK_TILES
+            ab = ab_next
+            if g + 1 < SLICES:
+                if i % PICK_TILES == PICK_TILES - 1:
+                    entity_picked.append(gather(entity_words, entity_list, g + 1, U32, "entity"))
+                if i == max(1, g * PICK_TILES):
+                    entity_scales.append(gather(entity_plane, entity_list, g + 1, U8, "scales_even" if g % 2 else "scales_odd"))
+            if i + AHEAD == 2 * PICK_TILES:
+                relation_scales.append(gather(relation_plane, relation_list, SLICES - 1, U8, "scales1"))
             if i + 1 < TILES:
-                ab = entity(i + 1)
-            if i + 3 < TILES:
-                cds.append(relation(i + 3))
-            prod = products(ab_now, cds[i], i)
-            for tag, bufs in [("y_bank", 1), ("cd_bank", 2)][: 1 if i < 13 else 2]:
-                if waiting and waiting[0][0] + 2 <= i:
-                    score(*waiting[0][1:], tag, bufs)
+                ab_next = entity(i + 1)
+            if i + AHEAD < TILES:
+                cds.append(relation(i + AHEAD))
+            prod = products(ab, cds[i], i)
+            for bank_name, bufs in [("y_bank", 1), ("cd_bank", 2)][: 1 if i + AHEAD < TILES else 2]:
+                if waiting and waiting[0][0] + SCORE_LAG <= i:
+                    score(*waiting[0][1:], bank_name, bufs)
                     waiting = waiting[1:]
             if place == 0:
                 h_bf16 = ring.tile([P, 2, n_tiles * P, PACK], BF16, name="h_bf16", align_bytes=64)
-            turn_and_add(prod, h_bf16, place, i)
-            if i == 1:
-                nr_q = quantise_weight(nr_raw, "nr", "spare0")
-            if i == 2:
-                ni_q = quantise_weight(ni_raw, "ni", "spare1")
+            add_and_turn(prod, h_bf16[:, :, place * P : (place + 1) * P, :], i)
+            if i == LENDING_TILES[0] + 1:
+                nr_q = quantise_weight(nr_raw, "nr", "lent0")
+            if i == LENDING_TILES[1] + 1:
+                ni_q = quantise_weight(ni_raw, "ni", "lent1")
             if place == n_tiles - 1:
                 width = n_tiles * P
                 h_q = quantise_h(h_bf16, width)
-                count = 512 // width
-                waiting.extend([(i, h_q, (i + 1) * P - width, width, first, count) for first in range(0, N // P, count)])
+                waiting.extend([(i, h_q, (i + 1) * P - width, width, first) for first in range(0, N // P, BANK // width)])
         for job in waiting:
             score(*job[1:], "cd_bank", 2)

@@ -70,6 +70,10 @@ def tile_list_ckg_bias_kernel(
             nc.sync.dma_start(out=raw[:], in_=weight.rearrange("(p i) c -> p i c", i=PACK))
             return raw
 
+        warm = keep.tile([P, 2], F32, name="warm")
+        nc.gpsimd.memset(warm[:], 0.0)
+        nc.scalar.activation(out=warm[:, 1:2], in_=warm[:, 0:1], func=IDENTITY, bias=warm[:, 0:1])
+
         nc.vector.memset(relation_plane[:].bitcast(I32), 0)
         nc.vector.memset(wr_planes[:].bitcast(I32), 0)
         nc.vector.memset(entity_plane[:].bitcast(I32), 0)
@@ -111,7 +115,7 @@ def tile_list_ckg_bias_kernel(
             )
             return codes, plane
 
-        relation_scales = [gather(relation_plane, relation_list, g, U8, "scales%d" % g) for g in range(SLICES - 1)]
+        relation_scales = [gather(relation_plane, relation_list, g, U8, "scales%d" % g) for g in range(SLICES)]
         relation_picked = [gather(relation_words, relation_list, g, U32, "relation%d" % g) for g in range(SLICES)]
         entity_scales = [gather(entity_plane, entity_list, 0, U8, "scales_even")]
         wer_q = quantise_weight(wer_raw, "wer", "lent0")
@@ -256,8 +260,6 @@ def tile_list_ckg_bias_kernel(
                     entity_picked.append(gather(entity_words, entity_list, g + 1, U32, "entity"))
                 if i == max(1, g * PICK_TILES):
                     entity_scales.append(gather(entity_plane, entity_list, g + 1, U8, "scales_even" if g % 2 else "scales_odd"))
-            if i + AHEAD == 2 * PICK_TILES:
-                relation_scales.append(gather(relation_plane, relation_list, SLICES - 1, U8, "scales1"))
             if i + 1 < TILES:
                 ab_next = entity(i + 1)
             if i + AHEAD < TILES:

from contextlib import ExitStack

import concourse.mybir as mybir
from concourse.masks import make_identity

K, L, R, N, T, J = 512, 512, 512, 512, 4096, 2048
FLOPS = 2 * J * (2 * K * R + 2 * L * R + 2 * R * N)

F32 = mybir.dt.float32
BF16 = mybir.dt.bfloat16
I32 = mybir.dt.int32
U32 = mybir.dt.uint32
U16 = mybir.dt.uint16
U8 = mybir.dt.uint8
FP8X4 = mybir.dt.float8_e4m3fn_x4
FP4X4 = mybir.dt.float4_e2m1fn_x4
MULT = mybir.AluOpType.mult
ADD = mybir.AluOpType.add
SUBTRACT = mybir.AluOpType.subtract
COPY = mybir.ActivationFunctionType.Copy
IDENTITY = mybir.ActivationFunctionType.Identity

P = 128
PACK = 4
BANK = 512
PICK = 512
PICK_TILES = PICK // P
SLICES = J // PICK
TILES = J // P
CHUNK_TILES = (4, 4, 4, 2, 1, 1)
AHEAD = 2
SCORE_LAG = 2
VECTOR_SUM_FROM = 6
VECTOR_SUM_EVERY = 3
LENDING_TILES = (2, 3)


def tile_list_ckg_bias_kernel(
    tc, tab_words, tab_scales, tab2_words, tab2_scales, wer, wei, wrr_words, wrr_scales,
    wri_words, wri_scales, nr, ni, b, offs, offs2, out
):
    nc = tc.nc
    with ExitStack() as ctx:
        keep = ctx.enter_context(tc.tile_pool(name="keep", bufs=1))
        ring = ctx.enter_context(tc.tile_pool(name="ring", bufs=2))
        psum = ctx.enter_context(tc.psum_pool(name="psum", bufs=1))

        entity_list = keep.tile([P, J // 16], U16, name="entity_list")
        relation_list = keep.tile([P, J // 16], U16, name="relation_list")
        relation_words = keep.tile([P, T], U32, name="relation_words", align_bytes=64)
        entity_plane = keep.tile([P, T], U8, name="entity_plane", align_bytes=64)
        relation_plane = keep.tile([P, T], U8, name="relation_plane", align_bytes=64)
        wrr_codes = keep.tile([P, 2 * R], U8, name="wrr_codes", align_bytes=64)
        wri_codes = keep.tile([P, 2 * R], U8, name="wri_codes", align_bytes=64)
        wr_planes = keep.tile([P, 2 * R], U8, name="wr_planes", align_bytes=64)
        identity = keep.tile([P, P], F32, name="identity", align_bytes=64)
        entity_words = keep.tile([P, T], U32, name="entity_words", align_bytes=64)

        def load_scale_rows(plane, rows, quadrant):
            nc.scalar.dma_start(
                out=plane.bitcast(I32)[32 * quadrant : 32 * quadrant + 4, :],
                in_=rows[0, 4 * quadrant : 4 * quadrant + 4, :].bitcast(I32),
            )

        def load_words(words, table):
            nc.sync.dma_start(out=words[:].bitcast(I32), in_=table[0].rearrange("p t i -> p (t i)").bitcast(I32))

        def load_rows(weight):
            raw = ring.tile([P, PACK, 512], F32, name="raw", align_bytes=64)
            nc.sync.dma_start(out=raw[:], in_=weight.rearrange("(p i) c -> p i c", i=PACK))
            return raw

        warm = keep.tile([P, 2], F32, name="warm")
        nc.gpsimd.memset(warm[:], 0.0)
        nc.scalar.activation(out=warm[:, 1:2], in_=warm[:, 0:1], func=IDENTITY, bias=warm[:, 0:1])

        nc.vector.memset(relation_plane[:].bitcast(I32), 0)
        nc.vector.memset(wr_planes[:].bitcast(I32), 0)
        nc.vector.memset(entity_plane[:].bitcast(I32), 0)
        make_identity(nc, identity[:])

        nc.sync.dma_start(relation_list[:], offs2)
        nc.sync.dma_start(entity_list[:], offs)
        nc.sync.dma_start(out=wrr_codes[:].bitcast(I32), in_=wrr_words[0].bitcast(I32))
        nc.sync.dma_start(out=wri_codes[:].bitcast(I32), in_=wri_words[0].bitcast(I32))
        load_words(relation_words, tab2_words)
        for quadrant in range(4):
            load_scale_rows(relation_plane[:], tab2_scales, quadrant)
        wer_raw = load_rows(wer)
        wei_raw = load_rows(wei)
        for quadrant in range(4):
            load_scale_rows(wr_planes[:, 0:R], wrr_scales, quadrant)
            load_scale_rows(wr_planes[:, R : 2 * R], wri_scales, quadrant)
        for quadrant in range(4):
            load_scale_rows(entity_plane[:], tab_scales, quadrant)
        load_words(entity_words, tab_words)

        def gather(window, offsets, g, dtype, buffer):
            picked = ring.tile([P, PICK], dtype, name=buffer, bufs=1, align_bytes=64)
            nc.vector.tensor_copy(picked[:], window[:].indirect(offsets[:, g * (PICK // 16) : (g + 1) * (PICK // 16)]))
            return picked

        def quantise_weight(raw, name, buffer):
            grouped = ring.tile([P, 512, PACK], BF16, name=buffer, bufs=1, align_bytes=64)
            for half in range(2):
                cols = slice(256 * half, 256 * (half + 1))
                nc.scalar.copy(
                    out=grouped[:, cols, :].rearrange("p (c e) i -> p c i e", e=4),
                    in_=raw[:, :, cols].rearrange("p i (c e) -> p c i e", e=4),
                )
            codes = keep.tile([P, 512], U32, name=name + "_codes", align_bytes=64)
            plane = keep.tile([P, 512], U8, name=name + "_plane", align_bytes=64)
            nc.vector.quantize_mx(
                out=codes[:].bitcast(FP8X4), scales=plane[:], in_=grouped[:].rearrange("p c i -> p (c i)")
            )
            return codes, plane

        relation_scales = [gather(relation_plane, relation_list, g, U8, "scales%d" % g) for g in range(SLICES)]
        relation_picked = [gather(relation_words, relation_list, g, U32, "relation%d" % g) for g in range(SLICES)]
        entity_scales = [gather(entity_plane, entity_list, 0, U8, "scales_even")]
        wer_q = quantise_weight(wer_raw, "wer", "lent0")
        wei_q = quantise_weight(wei_raw, "wei", "lent1")
        nr_raw = load_rows(nr)
        ni_raw = load_rows(ni)
        bias = ring.tile([P, N // P], F32, name="bias", bufs=1, align_bytes=64)
        with nc.allow_non_contiguous_dma(reason="one bias value a partition"):
            nc.sync.dma_start(out=bias[:], in_=b.rearrange("(c p) -> p c", p=P))
        entity_picked = [gather(entity_words, entity_list, 0, U32, "entity")]

        def sums_on_vector(i):
            return i >= VECTOR_SUM_FROM and i % VECTOR_SUM_EVERY == 0

        def project(words, scales, i, weight, weight_plane, bank_name, bufs):
            cols = slice((i % PICK_TILES) * P, (i % PICK_TILES + 1) * P)
            bank = psum.tile([P, R], F32, name=bank_name, bufs=bufs)
            nc.tensor.matmul_mx(
                out=bank[:], lhsT=words[i // PICK_TILES][:, cols].bitcast(FP8X4), lhsT_scale=scales[i // PICK_TILES][:, cols],
                rhs=weight, rhs_scale=weight_plane, start=True, stop=True,
            )
            return bank

        def entity(i):
            return [
                project(entity_picked, entity_scales, i, codes[:].bitcast(FP8X4), plane[:], "ab_bank", 3)
                for codes, plane in (wer_q, wei_q)
            ]

        def from_bank(bank, i):
            if sums_on_vector(i):
                return bank[:].rearrange("p (m u e) -> p u m e", u=2, e=2)
            return bank[:].rearrange("p (m t) -> p t m", t=PACK)

        def as_stored(row, i):
            if sums_on_vector(i):
                return row.rearrange("p (u m e) -> p u m e", u=2, e=2)
            return row.rearrange("p (t m) -> p t m", t=PACK)

        def relation(i):
            if i == 0:
                cd = ring.tile([P, 2, R], F32, name="scales_odd", bufs=1, align_bytes=64)
            else:
                cd = ring.tile([P, 2, R], F32, name="cd", bufs=AHEAD + 1, align_bytes=64)
            for part, codes in enumerate((wrr_codes, wri_codes)):
                bank = project(
                    relation_picked, relation_scales, i, codes[:].bitcast(FP4X4),
                    wr_planes[:, part * R : (part + 1) * R], "cd_bank", 2,
                )
                nc.scalar.copy(out=as_stored(cd[:, part], i), in_=from_bank(bank, i))
            return cd

        def products(ab, cd, i):
            a_view, b_view = [from_bank(bank, i) for bank in ab]
            if i in LENDING_TILES:
                prod = ring.tile([P, 4, R], F32, name="lent%d" % LENDING_TILES.index(i), bufs=1, align_bytes=64)
            else:
                prod = ring.tile([P, 4, R], F32, name="prod", bufs=3, align_bytes=64)
            if sums_on_vector(i):
                for term, (view, part) in enumerate(((a_view, 0), (a_view, 1), (b_view, 0), (b_view, 1))):
                    nc.vector.tensor_tensor(out=as_stored(prod[:, term], i), in0=view, in1=as_stored(cd[:, part], i), op=MULT)
            else:
                nc.vector.scalar_tensor_tensor(
                    out=as_stored(prod[:, 0], i), in0=a_view, scalar=-1.0, in1=as_stored(cd[:, 0], i), op0=MULT, op1=MULT
                )
                nc.vector.tensor_tensor(out=as_stored(prod[:, 1], i), in0=a_view, in1=as_stored(cd[:, 1], i), op=MULT)
                nc.vector.tensor_tensor(
                    out=prod[:, 2:4].rearrange("p s (t m) -> p s t m", t=PACK),
                    in0=b_view.unsqueeze(1).to_broadcast([P, 2, PACK, P]),
                    in1=cd[:].rearrange("p s (t m) -> p s t m", t=PACK), op=MULT,
                )
            return prod

        def add_and_turn(prod, h_slot, i):
            if sums_on_vector(i):
                h_rows = ring.tile([P, 2, R], BF16, name="h_rows", align_bytes=64)
                nc.vector.tensor_tensor(out=h_rows[:, 1], in0=prod[:, 1], in1=prod[:, 2], op=ADD)
                nc.vector.tensor_tensor(out=h_rows[:, 0], in0=prod[:, 0], in1=prod[:, 3], op=SUBTRACT)
                pairs = h_rows[:].rearrange("p s r -> p (s r)").bitcast(F32)
                bank = psum.tile([P, PACK, P], F32, name="h_bank", bufs=2)
                for block in range(4):
                    nc.tensor.transpose(bank[:, block, :], pairs[:, block * P : (block + 1) * P], identity[:])
                nc.scalar.copy(out=h_slot.bitcast(F32), in_=bank[:].rearrange("p (s u) j -> p s j u", u=2))
                return
            for part, (terms, sign) in enumerate((((3, 0), -1.0), ((2, 1), 1.0))):
                bank = psum.tile([P, PACK, P], F32, name="h_bank", bufs=2)
                for n_term, term in enumerate(terms):
                    for t in range(PACK):
                        nc.tensor.matmul(
                            bank[:, t, :], lhsT=prod[:, term, t * P : (t + 1) * P], rhs=identity[:], is_transpose=True,
                            start=(n_term == 0 and t == 0), stop=(n_term == 1 and t == PACK - 1),
                        )
                nc.scalar.activation(out=h_slot[:, part], in_=bank[:].rearrange("p t j -> p j t"), func=COPY, scale=sign)

        def quantise_h(h_bf16, width):
            codes = ring.tile([P, 2, width], U32, name="h_codes", bufs=3, align_bytes=64)
            plane = ring.tile([P, 2, width], U8, name="h_plane", bufs=3, align_bytes=64)
            nc.vector.quantize_mx(
                out=codes[:].rearrange("p s j -> p (s j)").bitcast(FP8X4), scales=plane[:].rearrange("p s j -> p (s j)"),
                in_=h_bf16[:].rearrange("p s j t -> p (s j t)"),
            )
            return codes, plane

        def score(h_q, j0, width, first, bank_name, bufs):
            count = BANK // width
            bank = psum.tile([P, count, width], F32, name=bank_name, bufs=bufs)
            for c in range(count):
                cols = slice((first + c) * P, (first + c + 1) * P)
                for part, (codes, plane) in enumerate((nr_q, ni_q)):
                    nc.tensor.matmul_mx(
                        out=bank[:, c, :], lhsT=codes[:, cols].bitcast(FP8X4), lhsT_scale=plane[:, cols],
                        rhs=h_q[0][:, part, :].bitcast(FP8X4), rhs_scale=h_q[1][:, part, :],
                        start=(part == 0), stop=(part == 1),
                    )
            y = ring.tile([P, count, width], F32, name="y", bufs=4, align_bytes=64)
            if j0 + width < J:
                for c in range(count):
                    nc.scalar.activation(
                        out=y[:, c, :], in_=bank[:, c, :], func=IDENTITY, bias=bias[:, first + c : first + c + 1]
                    )
            else:
                nc.vector.tensor_tensor(
                    out=y[:], in0=bank[:], in1=bias[:, first : first + count].unsqueeze(2).to_broadcast([P, count, width]), op=ADD
                )
            nc.sync.dma_start(
                out=out[first * P : (first + count) * P, j0 : j0 + width].rearrange("(c p) j -> p c j", p=P), in_=y[:]
            )

        place_of = []
        for n_tiles in CHUNK_TILES:
            place_of.extend([(place, n_tiles) for place in range(n_tiles)])

        waiting = []
        cds = [relation(i) for i in range(AHEAD)]
        ab_next = entity(0)
        for i in range(TILES):
            place, n_tiles = place_of[i]
            g = i // PICK_TILES
            ab = ab_next
            if g + 1 < SLICES:
                if i % PICK_TILES == PICK_TILES - 1:
                    entity_picked.append(gather(entity_words, entity_list, g + 1, U32, "entity"))
                if i == max(1, g * PICK_TILES):
                    entity_scales.append(gather(entity_plane, entity_list, g + 1, U8, "scales_even" if g % 2 else "scales_odd"))
            if i + 1 < TILES:
                ab_next = entity(i + 1)
            if i + AHEAD < TILES:
                cds.append(relation(i + AHEAD))
            prod = products(ab, cds[i], i)
            for bank_name, bufs in [("y_bank", 1), ("cd_bank", 2)][: 1 if i + AHEAD < TILES else 2]:
                if waiting and waiting[0][0] + SCORE_LAG <= i:
                    score(*waiting[0][1:], bank_name, bufs)
                    waiting = waiting[1:]
            if place == 0:
                h_bf16 = ring.tile([P, 2, n_tiles * P, PACK], BF16, name="h_bf16", align_bytes=64)
            add_and_turn(prod, h_bf16[:, :, place * P : (place + 1) * P, :], i)
            if i == LENDING_TILES[0] + 1:
                nr_q = quantise_weight(nr_raw, "nr", "lent0")
            if i == LENDING_TILES[1] + 1:
                ni_q = quantise_weight(ni_raw, "ni", "lent1")
            if place == n_tiles - 1:
                width = n_tiles * P
                h_q = quantise_h(h_bf16, width)
                waiting.extend([(i, h_q, (i + 1) * P - width, width, first) for first in range(0, N // P, BANK // width)])
        for job in waiting:
            score(*job[1:], "cd_bank", 2)
